import numpy as np
import ml_dtypes


def mxq(x, axis, fmt="e4m3"):
    dtype, down = {"e4m3": (ml_dtypes.float8_e4m3fn, 7), "e5m2": (ml_dtypes.float8_e5m2, 14)}[fmt]
    v = np.moveaxis(np.asarray(x, np.float32).astype(ml_dtypes.bfloat16).astype(np.float64), axis, -1)
    blocks = v.reshape(v.shape[:-1] + (-1, 32))
    amax = np.abs(blocks).max(-1, keepdims=True)
    byte = np.maximum(np.where(amax > 0, np.frexp(amax)[1] - 1 + 127, 0) - down, 1)
    scale = np.exp2(byte - 127.0)
    codes = (blocks / scale).astype(np.float32).astype(dtype).astype(np.float64)
    return np.moveaxis((codes * scale).reshape(v.shape), -1, axis)


WIDE = False


def mx_kscale(k):
    if not WIDE:
        return np.ones(k)
    levels = np.array([10, -10, 5, -5, 0])
    if k % 512:
        return np.exp2(np.random.permutation(np.resize(levels, k // 32))).repeat(32)
    a = np.empty((k // 512, 16))
    for p in range(k // 512):
        a[p, :8] = np.random.permutation(np.resize(levels, 8))
        for g in range(8):
            far = levels[np.abs(levels - a[p, g]) >= 10]
            a[p, g + 8] = far[np.random.randint(len(far))]
    return np.exp2(a.ravel()).repeat(32)


def f64(x):
    return np.asarray(x).astype(np.float64)


def striped(idx):
    return np.tile(np.asarray(idx).reshape(-1, 16).T, (8, 1)).astype(np.uint16)


def unstriped(offs):
    return offs[:16].T.reshape(-1).astype(np.int64)


def striped8(idx):
    return np.asarray(idx).reshape(8, -1, 16).transpose(0, 2, 1).reshape(128, -1).astype(np.uint16)


def unstriped8(offs):
    return offs.reshape(8, 16, -1).transpose(0, 2, 1).reshape(8, -1).astype(np.int64)


def pick8(x, idx, run):
    r = np.arange(len(x))
    return x[r[:, None], idx[r % (8 * run) // run]]


E2M1 = np.array([0.0, 0.5, 1.0, 1.5, 2.0, 3.0, 4.0, 6.0, -0.0, -0.5, -1.0, -1.5, -2.0, -3.0, -4.0, -6.0])


def pack_weight(w, fmt):
    k, n = w.shape
    w = f64(np.asarray(w, np.float32).astype(ml_dtypes.bfloat16)).reshape(k // 32, 32, n)
    amax = np.abs(w).max(1)
    if fmt == "e4m3":
        byte = np.frexp(amax)[1] - 1 + 127 - 7
    else:
        mant, ex = np.frexp(amax / 6.0)
        byte = np.where(mant > 0.5, ex, ex - 1) + 127
    byte = np.clip(np.where(amax > 0, byte, 1), 1, 254)
    scaled = (w * np.exp2(127.0 - byte)[:, None, :]).reshape(k, n).astype(np.float32)
    by_word = np.ascontiguousarray(scaled.reshape(k // 512, 128, 4, n).transpose(0, 1, 3, 2))
    if fmt == "e4m3":
        words = by_word.astype(ml_dtypes.float8_e4m3fn).view(np.uint8)
    else:
        c = by_word.astype(ml_dtypes.float4_e2m1fn).view(np.uint8) & 0xF
        words = (c[..., 0::2] | (c[..., 1::2] << 4)).reshape(k // 512, 128, 2 * n)
    return np.ascontiguousarray(words), np.ascontiguousarray(byte.astype(np.uint8).reshape(k // 512, 16, n))


def unpack_weight(words, scales, fmt):
    g, _, n = scales.shape
    words = np.ascontiguousarray(words).reshape(g, 128, n, -1)
    if fmt == "e4m3":
        vals = words.view(ml_dtypes.float8_e4m3fn).astype(np.float64)
    else:
        nib = np.empty((g, 128, n, 4), np.uint8)
        nib[..., 0::2] = words & 0xF
        nib[..., 1::2] = words >> 4
        vals = E2M1[nib]
    vals = vals * np.repeat(np.exp2(scales.astype(np.float64) - 127.0), 8, axis=1)[..., None]
    return vals.transpose(0, 1, 3, 2).reshape(g * 512, n)


K, J, R, T, U, F, G, O, D, N, S = 512, 256, 512, 512, 512, 2048, 1024, 128, 512, 256, 1024


def setup_inputs():
    n = np.random.standard_normal
    idx = np.stack([np.random.permutation(T)[:J] for _ in range(8)])
    idx2 = np.stack([np.random.permutation(U)[:J] for _ in range(8)])
    idx3 = np.stack([np.random.permutation(F)[:G] for _ in range(8)])
    idx4 = np.random.permutation(G)[:R]
    idx5 = np.stack([np.random.permutation(J)[:O] for _ in range(8)])
    idx6 = np.stack([np.random.permutation(D)[:O] for _ in range(8)])
    idx7 = np.random.permutation(S)[:N]
    fk = mx_kscale(K)
    fr = mx_kscale(R)
    vsp = pack_weight(n((R, S)) * 1 / np.sqrt(R) / fr[:, None], "e4m3")
    return {
        "ta": (np.random.randint(-7, 8, (K, T)).astype(np.float64)).astype(np.float32),
        "tb": (np.random.randint(-7, 8, (K, U)).astype(np.float64)).astype(np.float32),
        "ga": ((np.random.randint(8, 25, (K, 1)) / 64.0) * fk[:, None]).astype(np.float32),
        "gb": ((np.random.randint(8, 25, (K, 1)) / 64.0) * fk[:, None]).astype(np.float32),
        "ua": (np.random.randint(-7, 8, (K, F)).astype(np.float64)).astype(np.float32),
        "ha": ((np.random.randint(8, 25, (K, 1)) / 1024.0) / fk[:, None]).astype(np.float32),
        "hb": (np.random.uniform(0.5, 1.6, (K, 1))).astype(np.float32),
        "tl": (np.random.randint(1, 9, (R, D)).astype(np.float64)).astype(np.float32),
        "sa": (np.random.uniform(0.5, 1.6, (R, 1)) * fr[:, None]).astype(np.float32),
        "sl": (np.random.uniform(0.1, 0.4, (R, 1))).astype(np.float32),
        "vs_words": vsp[0],
        "vs_scales": vsp[1],
        "offs": striped8(idx),
        "offs2": striped8(idx2),
        "offs3": striped8(idx3),
        "offs4": striped(idx4),
        "offs5": striped8(idx5),
        "offs6": striped8(idx6),
        "offs7": striped(idx7),
    }


def reference(ta, tb, ga, gb, ua, ha, hb, tl, sa, sl, vs_words, vs_scales, offs, offs2, offs3, offs4, offs5, offs6, offs7):
    idx = unstriped8(offs)
    idx2 = unstriped8(offs2)
    idx3 = unstriped8(offs3)
    idx4 = unstriped(offs4)
    idx5 = unstriped8(offs5)
    idx6 = unstriped8(offs6)
    idx7 = unstriped(offs7)
    vsu = unpack_weight(vs_words, vs_scales, "e4m3")
    xc = np.maximum(pick8(f64(ta), idx, 64) * f64(ga), pick8(f64(tb), idx2, 64) * f64(gb))
    wcd = pick8(f64(ua), idx3, 64) * f64(ha)
    wc = wcd[:, idx4] * f64(hb)
    wcq = mxq(wc, 0, "e4m3")
    xcq = mxq(xc, 0, "e4m3")
    a = wcq.T @ xcq
    hid = pick8(a, idx5, 64) * f64(sa) * pick8(f64(tl), idx6, 64) * f64(sl)
    vsidx7g = vsu[:, idx7]
    hidq = mxq(hid, 0, "e4m3")
    y = vsidx7g.T @ hidq
    return y

@@ -1,0 +1,177 @@
+from contextlib import ExitStack
+
+import concourse.mybir as mybir
+
+K, J, R, T, U, F, G, O, D, N, S = 512, 256, 512, 512, 512, 2048, 1024, 128, 512, 256, 1024
+FLOPS = 2 * K * R * J + 2 * R * N * O
+
+F32 = mybir.dt.float32
+BF16 = mybir.dt.bfloat16
+I32 = mybir.dt.int32
+U32 = mybir.dt.uint32
+U16 = mybir.dt.uint16
+U8 = mybir.dt.uint8
+FP8X4 = mybir.dt.float8_e4m3fn_x4
+COPY = mybir.ActivationFunctionType.Copy
+MAX = mybir.AluOpType.max
+MULT = mybir.AluOpType.mult
+
+P = 128
+PACK = 4
+HALF = J // 2
+
+
+def tile_picked_largercode_respelled_one_codedgain_store_plain_kernel(
+    tc, ta, tb, ga, gb, ua, ha, hb, tl, sa, sl, vs_words, vs_scales,
+    offs, offs2, offs3, offs4, offs5, offs6, offs7, out,
+):
+    nc = tc.nc
+    with ExitStack() as ctx:
+        keep = ctx.enter_context(tc.tile_pool(name="keep", bufs=1))
+        psum = ctx.enter_context(tc.psum_pool(name="psum", bufs=1))
+
+        def load_list(src, name):
+            tile = keep.tile(list(src.shape), U16, name=name)
+            nc.sync.dma_start(tile[:], src)
+            return tile
+
+        def load_steps(queue, src, name, tag=None, cols=slice(0, PACK)):
+            tile = keep.tile([P, cols.stop - cols.start], F32, name=name, tag=tag or name)
+            queue.dma_start(tile[:], src.rearrange("(p t) o -> p (t o)", t=PACK)[:, cols])
+            return tile
+
+        def load_plane(src, t, name):
+            tile = keep.tile([P, src.shape[1]], F32, name=name)
+            nc.sync.dma_start(tile[:], src.rearrange("(p t) c -> t p c", t=PACK)[t])
+            return tile
+
+        def gather(dst, window, offsets, steps, t):
+            nc.scalar.activation(dst, window[:].indirect(offsets), COPY, scale=steps[:, t : t + 1])
+
+        scale_win = keep.tile([P, S], U8, name="scale_win")
+        nc.gpsimd.memset(scale_win[:].bitcast(I32), 0)
+
+        ta_p = [load_plane(ta, 0, "ta0")]
+        l1 = load_list(offs, "l1")
+        ga_t = load_steps(nc.scalar, ga, "ga_t", tag="ga_then_xb")
+        ha_t = load_steps(nc.scalar, ha, "ha_t")
+        ua_p = [load_plane(ua, 0, "ua0")]
+        l3 = load_list(offs3, "l3")
+        ua_p.append(load_plane(ua, 1, "ua1"))
+        l4 = load_list(offs4, "l4")
+        hb_t = [load_steps(nc.sync, hb, "hb_lo", cols=slice(0, 2))]
+        ua_p.extend(load_plane(ua, t, "ua%d" % t) for t in range(2, PACK))
+        hb_t.append(load_steps(nc.sync, hb, "hb_hi", cols=slice(2, 4)))
+        l7 = load_list(offs7, "l7")
+        word_win = keep.tile([P, S], I32, name="word_win")
+        nc.sync.dma_start(word_win[:], vs_words[0].rearrange("p s b -> p (s b)").bitcast(I32))
+        for q in range(4):
+            nc.sync.dma_start(
+                scale_win[32 * q : 32 * q + 4, :].bitcast(I32),
+                vs_scales[0, 4 * q : 4 * q + 4, :].bitcast(I32),
+            )
+        l2 = load_list(offs2, "l2")
+        gb_t = load_steps(nc.sync, gb, "gb_t")
+        tb_p = [load_plane(tb, t, "tb%d" % t) for t in range(PACK)]
+        ta_p.extend(load_plane(ta, t, "ta%d" % t) for t in range(1, PACK))
+        l6 = load_list(offs6, "l6")
+        sl_t = load_steps(nc.sync, sl, "sl_t")
+        tl_p = [load_plane(tl, t, "tl%d" % t) for t in range(PACK)]
+        l5 = load_list(offs5, "l5")
+        sa_t = load_steps(nc.sync, sa, "sa_t")
+
+        xa = keep.tile([P, PACK, J], F32, name="xa")
+        gather(xa[:, 0, :], ta_p[0], l1[:], ga_t, 0)
+
+        vs_codes = keep.tile([P, N], U32, name="vs_codes", align_bytes=64)
+        vs_planes = keep.tile([P, N], U8, name="vs_planes", align_bytes=64)
+        nc.vector.tensor_copy(vs_codes[:], word_win[:].bitcast(U32).indirect(l7[:]))
+        nc.vector.tensor_copy(vs_planes[:], scale_win[:].indirect(l7[:]))
+
+        wc = keep.tile([P, PACK, R], BF16, name="wc")
+        wcd = [keep.tile([P, G], F32, name="wcd%d" % t) for t in range(PACK)]
+        for pair in range(2):
+            for e in range(2):
+                gather(wcd[2 * pair + e][:], ua_p[2 * pair + e], l3[:], ha_t, 2 * pair + e)
+            for e in range(2):
+                gather(wc[:, 2 * pair + e, :], wcd[2 * pair + e], l4[:], hb_t[pair], e)
+        wc_il = keep.tile([P, R * PACK], BF16, name="wc_il", align_bytes=64)
+        nc.vector.tensor_copy(
+            wc_il[:].rearrange("p (s m i t) -> p m s i t", s=PACK, i=2, t=PACK),
+            wc[:].rearrange("p t (m i s) -> p m s i t", i=2, s=PACK),
+        )
+        wc_codes = keep.tile([P, R], U32, name="wc_codes", align_bytes=64)
+        wc_scales = keep.tile([P, R], U8, name="wc_scales", align_bytes=64)
+        nc.vector.quantize_mx(wc_codes[:].bitcast(FP8X4), wc_scales[:], wc_il[:])
+
+        for t in range(1, PACK):
+            gather(xa[:, t, :], ta_p[t], l1[:], ga_t, t)
+        xb = keep.tile([P, 2, PACK, HALF], F32, name="xb", tag="ga_then_xb")
+        a_win = [keep.tile([P, J], F32, name="a%d" % s) for s in range(PACK)]
+        a_ps = {}
+        for h in range(2):
+            cols = slice(h * HALF, (h + 1) * HALF)
+            for t in range(PACK):
+                gather(xb[:, h, t, :], tb_p[t], l2[:, h * HALF // 16 : (h + 1) * HALF // 16], gb_t, t)
+            xc_il = keep.tile([P, HALF * PACK], BF16, name="xc_il%d" % h, align_bytes=64)
+            nc.vector.tensor_tensor(
+                xc_il[:].rearrange("p (c i t) -> p c t i", i=4, t=PACK),
+                xa[:, :, cols].rearrange("p t (c i) -> p c t i", i=4),
+                xb[:, h, :, :].rearrange("p t (c i) -> p c t i", i=4),
+                MAX,
+            )
+            xc_codes = keep.tile([P, HALF], U32, name="xc_codes%d" % h, align_bytes=64)
+            xc_scales = keep.tile([P, HALF], U8, name="xc_scales%d" % h, align_bytes=64)
+            nc.vector.quantize_mx(xc_codes[:].bitcast(FP8X4), xc_scales[:], xc_il[:])
+            for s in range(PACK):
+                acc = psum.tile([P, HALF], F32, name="acc%d%d" % (h, s), tag="bank%d" % (PACK * h + s))
+                nc.tensor.matmul_mx(
+                    acc[:],
+                    lhsT=wc_codes[:, s * P : (s + 1) * P].bitcast(FP8X4),
+                    lhsT_scale=wc_scales[:, s * P : (s + 1) * P],
+                    rhs=xc_codes[:].bitcast(FP8X4),
+                    rhs_scale=xc_scales[:],
+                    start=True,
+                    stop=True,
+                )
+                a_ps[(h, s)] = acc
+
+        gain = keep.tile([P, PACK, O], F32, name="gain")
+        for s in range(PACK):
+            gather(gain[:, s, :], tl_p[s], l6[:], sl_t, s)
+
+        picked = keep.tile([P, PACK, O], F32, name="picked")
+        for s in range(PACK):
+            for h in range(2):
+                nc.vector.tensor_copy(a_win[s][:, h * HALF : (h + 1) * HALF], a_ps[(h, s)][:])
+            gather(picked[:, s, :], a_win[s], l5[:], sa_t, s)
+
+        hid_il = keep.tile([P, O * PACK], BF16, name="hid_il", align_bytes=64)
+        nc.vector.tensor_tensor(
+            hid_il[:].rearrange("p (c i t) -> p c t i", i=4, t=PACK),
+            picked[:].rearrange("p t (c i) -> p c t i", i=4),
+            gain[:].rearrange("p t (c i) -> p c t i", i=4),
+            MULT,
+        )
+        hid_codes = keep.tile([P, O], U32, name="hid_codes", align_bytes=64)
+        hid_scales = keep.tile([P, O], U8, name="hid_scales", align_bytes=64)
+        nc.vector.quantize_mx(hid_codes[:].bitcast(FP8X4), hid_scales[:], hid_il[:])
+
+        for b in range(N // P):
+            acc = psum.tile([P, O], F32, name="y%d" % b, tag="bank%d" % b)
+            nc.tensor.matmul_mx(
+                acc[:],
+                lhsT=vs_codes[:, b * P : (b + 1) * P].bitcast(FP8X4),
+                lhsT_scale=vs_planes[:, b * P : (b + 1) * P],
+                rhs=hid_codes[:].bitcast(FP8X4),
+                rhs_scale=hid_scales[:],
+                start=True,
+                stop=True,
+            )
+            res = keep.tile([P, O], F32, name="res%d" % b)
+            if b == 0:
+                nc.vector.tensor_copy(res[:], acc[:])
+                nc.sync.dma_start(out[b * P : (b + 1) * P, :], res[:])
+            else:
+                nc.scalar.copy(res[:], acc[:])
+                nc.scalar.dma_start(out[b * P : (b + 1) * P, :], res[:])

@@ -35,8 +35,8 @@ def tile_picked_largercode_respelled_one_codedgain_store_plain_kernel(
             nc.sync.dma_start(tile[:], src)
             return tile
 
-        def load_steps(queue, src, name, tag=None, cols=slice(0, PACK)):
-            tile = keep.tile([P, cols.stop - cols.start], F32, name=name, tag=tag or name)
+        def load_steps(queue, src, name, cols=slice(0, PACK)):
+            tile = keep.tile([P, cols.stop - cols.start], F32, name=name)
             queue.dma_start(tile[:], src.rearrange("(p t) o -> p (t o)", t=PACK)[:, cols])
             return tile
 
@@ -49,36 +49,35 @@ def tile_picked_largercode_respelled_one_codedgain_store_plain_kernel(
             nc.scalar.activation(dst, window[:].indirect(offsets), COPY, scale=steps[:, t : t + 1])
 
         scale_win = keep.tile([P, S], U8, name="scale_win")
-        nc.gpsimd.memset(scale_win[:].bitcast(I32), 0)
+        nc.vector.memset(scale_win[:].bitcast(I32), 0)
 
         ta_p = [load_plane(ta, 0, "ta0")]
         l1 = load_list(offs, "l1")
-        ga_t = load_steps(nc.scalar, ga, "ga_t", tag="ga_then_xb")
+        ga_t = load_steps(nc.scalar, ga, "ga_t")
         ha_t = load_steps(nc.scalar, ha, "ha_t")
-        ua_p = [load_plane(ua, 0, "ua0")]
         l3 = load_list(offs3, "l3")
-        ua_p.append(load_plane(ua, 1, "ua1"))
+        ua_p = [load_plane(ua, t, "ua%d" % t) for t in range(2)]
         l4 = load_list(offs4, "l4")
-        hb_t = [load_steps(nc.sync, hb, "hb_lo", cols=slice(0, 2))]
-        ua_p.extend(load_plane(ua, t, "ua%d" % t) for t in range(2, PACK))
-        hb_t.append(load_steps(nc.sync, hb, "hb_hi", cols=slice(2, 4)))
-        l7 = load_list(offs7, "l7")
-        word_win = keep.tile([P, S], I32, name="word_win")
-        nc.sync.dma_start(word_win[:], vs_words[0].rearrange("p s b -> p (s b)").bitcast(I32))
+        hb_t = [load_steps(nc.gpsimd, hb, "hb_lo", cols=slice(0, 2))]
         for q in range(4):
-            nc.sync.dma_start(
+            nc.gpsimd.dma_start(
                 scale_win[32 * q : 32 * q + 4, :].bitcast(I32),
                 vs_scales[0, 4 * q : 4 * q + 4, :].bitcast(I32),
             )
-        l2 = load_list(offs2, "l2")
-        gb_t = load_steps(nc.sync, gb, "gb_t")
-        tb_p = [load_plane(tb, t, "tb%d" % t) for t in range(PACK)]
+        gb_t = load_steps(nc.gpsimd, gb, "gb_t")
+        sl_t = load_steps(nc.gpsimd, sl, "sl_t")
+        sa_t = load_steps(nc.gpsimd, sa, "sa_t")
+        ua_p.extend(load_plane(ua, t, "ua%d" % t) for t in range(2, PACK))
+        l7 = load_list(offs7, "l7")
+        word_win = keep.tile([P, S], I32, name="word_win")
+        nc.sync.dma_start(word_win[:], vs_words[0].rearrange("p s b -> p (s b)").bitcast(I32))
+        hb_t.append(load_steps(nc.sync, hb, "hb_hi", cols=slice(2, 4)))
         ta_p.extend(load_plane(ta, t, "ta%d" % t) for t in range(1, PACK))
+        tb_p = [load_plane(tb, t, "tb%d" % t) for t in range(PACK)]
+        l2 = load_list(offs2, "l2")
         l6 = load_list(offs6, "l6")
-        sl_t = load_steps(nc.sync, sl, "sl_t")
         tl_p = [load_plane(tl, t, "tl%d" % t) for t in range(PACK)]
         l5 = load_list(offs5, "l5")
-        sa_t = load_steps(nc.sync, sa, "sa_t")
 
         xa = keep.tile([P, PACK, J], F32, name="xa")
         gather(xa[:, 0, :], ta_p[0], l1[:], ga_t, 0)
@@ -106,18 +105,18 @@ def tile_picked_largercode_respelled_one_codedgain_store_plain_kernel(
 
         for t in range(1, PACK):
             gather(xa[:, t, :], ta_p[t], l1[:], ga_t, t)
-        xb = keep.tile([P, 2, PACK, HALF], F32, name="xb", tag="ga_then_xb")
+        xb = keep.tile([P, 2, PACK, HALF], F32, name="xb")
         a_win = [keep.tile([P, J], F32, name="a%d" % s) for s in range(PACK)]
         a_ps = {}
         for h in range(2):
             cols = slice(h * HALF, (h + 1) * HALF)
             for t in range(PACK):
                 gather(xb[:, h, t, :], tb_p[t], l2[:, h * HALF // 16 : (h + 1) * HALF // 16], gb_t, t)
-            xc_il = keep.tile([P, HALF * PACK], BF16, name="xc_il%d" % h, align_bytes=64)
+            xc_il = keep.tile([P, HALF * PACK], BF16, name="xc_il%d" % h, tag="xc_il", align_bytes=64)
             nc.vector.tensor_tensor(
-                xc_il[:].rearrange("p (c i t) -> p c t i", i=4, t=PACK),
-                xa[:, :, cols].rearrange("p t (c i) -> p c t i", i=4),
-                xb[:, h, :, :].rearrange("p t (c i) -> p c t i", i=4),
+                xc_il[:].rearrange("p (c i t) -> p c t i", i=2, t=PACK),
+                xa[:, :, cols].rearrange("p t (c i) -> p c t i", i=2),
+                xb[:, h, :, :].rearrange("p t (c i) -> p c t i", i=2),
                 MAX,
             )
             xc_codes = keep.tile([P, HALF], U32, name="xc_codes%d" % h, align_bytes=64)
@@ -148,9 +147,9 @@ def tile_picked_largercode_respelled_one_codedgain_store_plain_kernel(
 
         hid_il = keep.tile([P, O * PACK], BF16, name="hid_il", align_bytes=64)
         nc.vector.tensor_tensor(
-            hid_il[:].rearrange("p (c i t) -> p c t i", i=4, t=PACK),
-            picked[:].rearrange("p t (c i) -> p c t i", i=4),
-            gain[:].rearrange("p t (c i) -> p c t i", i=4),
+            hid_il[:].rearrange("p (c i t) -> p c t i", i=2, t=PACK),
+            picked[:].rearrange("p t (c i) -> p c t i", i=2),
+            gain[:].rearrange("p t (c i) -> p c t i", i=2),
             MULT,
         )
         hid_codes = keep.tile([P, O], U32, name="hid_codes", align_bytes=64)

@@ -19,6 +19,7 @@ MULT = mybir.AluOpType.mult
 P = 128
 PACK = 4
 HALF = J // 2
+OH = O // 2
 
 
 def tile_picked_largercode_respelled_one_codedgain_store_plain_kernel(
@@ -58,26 +59,26 @@ def tile_picked_largercode_respelled_one_codedgain_store_plain_kernel(
         l3 = load_list(offs3, "l3")
         ua_p = [load_plane(ua, t, "ua%d" % t) for t in range(2)]
         l4 = load_list(offs4, "l4")
-        hb_t = [load_steps(nc.gpsimd, hb, "hb_lo", cols=slice(0, 2))]
-        for q in range(4):
-            nc.gpsimd.dma_start(
-                scale_win[32 * q : 32 * q + 4, :].bitcast(I32),
-                vs_scales[0, 4 * q : 4 * q + 4, :].bitcast(I32),
-            )
-        gb_t = load_steps(nc.gpsimd, gb, "gb_t")
-        sl_t = load_steps(nc.gpsimd, sl, "sl_t")
-        sa_t = load_steps(nc.gpsimd, sa, "sa_t")
+        hb_t = [load_steps(nc.sync, hb, "hb_lo", cols=slice(0, 2))]
         ua_p.extend(load_plane(ua, t, "ua%d" % t) for t in range(2, PACK))
         l7 = load_list(offs7, "l7")
+        scale_rows = keep.tile([4, 4, S // 4], I32, name="scale_rows")
+        nc.sync.dma_start(scale_rows[:], vs_scales[0].bitcast(I32).rearrange("(q r) s -> r q s", r=4))
         word_win = keep.tile([P, S], I32, name="word_win")
         nc.sync.dma_start(word_win[:], vs_words[0].rearrange("p s b -> p (s b)").bitcast(I32))
         hb_t.append(load_steps(nc.sync, hb, "hb_hi", cols=slice(2, 4)))
         ta_p.extend(load_plane(ta, t, "ta%d" % t) for t in range(1, PACK))
+        gb_t = load_steps(nc.sync, gb, "gb_t")
         tb_p = [load_plane(tb, t, "tb%d" % t) for t in range(PACK)]
         l2 = load_list(offs2, "l2")
         l6 = load_list(offs6, "l6")
+        sl_t = load_steps(nc.sync, sl, "sl_t")
         tl_p = [load_plane(tl, t, "tl%d" % t) for t in range(PACK)]
         l5 = load_list(offs5, "l5")
+        sa_t = load_steps(nc.sync, sa, "sa_t")
+
+        for q in range(4):
+            nc.vector.tensor_copy(scale_win[32 * q : 32 * q + 4, :].bitcast(I32), scale_rows[:, q, :])
 
         xa = keep.tile([P, PACK, J], F32, name="xa")
         gather(xa[:, 0, :], ta_p[0], l1[:], ga_t, 0)
@@ -105,18 +106,18 @@ def tile_picked_largercode_respelled_one_codedgain_store_plain_kernel(
 
         for t in range(1, PACK):
             gather(xa[:, t, :], ta_p[t], l1[:], ga_t, t)
-        xb = keep.tile([P, 2, PACK, HALF], F32, name="xb")
+        xb = keep.tile([P, PACK, J], F32, name="xb")
         a_win = [keep.tile([P, J], F32, name="a%d" % s) for s in range(PACK)]
         a_ps = {}
         for h in range(2):
             cols = slice(h * HALF, (h + 1) * HALF)
             for t in range(PACK):
-                gather(xb[:, h, t, :], tb_p[t], l2[:, h * HALF // 16 : (h + 1) * HALF // 16], gb_t, t)
+                gather(xb[:, t, cols], tb_p[t], l2[:, h * HALF // 16 : (h + 1) * HALF // 16], gb_t, t)
             xc_il = keep.tile([P, HALF * PACK], BF16, name="xc_il%d" % h, tag="xc_il", align_bytes=64)
             nc.vector.tensor_tensor(
                 xc_il[:].rearrange("p (c i t) -> p c t i", i=2, t=PACK),
                 xa[:, :, cols].rearrange("p t (c i) -> p c t i", i=2),
-                xb[:, h, :, :].rearrange("p t (c i) -> p c t i", i=2),
+                xb[:, :, cols].rearrange("p t (c i) -> p c t i", i=2),
                 MAX,
             )
             xc_codes = keep.tile([P, HALF], U32, name="xc_codes%d" % h, align_bytes=64)
@@ -143,34 +144,41 @@ def tile_picked_largercode_respelled_one_codedgain_store_plain_kernel(
         for s in range(PACK):
             for h in range(2):
                 nc.vector.tensor_copy(a_win[s][:, h * HALF : (h + 1) * HALF], a_ps[(h, s)][:])
-            gather(picked[:, s, :], a_win[s], l5[:], sa_t, s)
-
-        hid_il = keep.tile([P, O * PACK], BF16, name="hid_il", align_bytes=64)
-        nc.vector.tensor_tensor(
-            hid_il[:].rearrange("p (c i t) -> p c t i", i=2, t=PACK),
-            picked[:].rearrange("p t (c i) -> p c t i", i=2),
-            gain[:].rearrange("p t (c i) -> p c t i", i=2),
-            MULT,
-        )
-        hid_codes = keep.tile([P, O], U32, name="hid_codes", align_bytes=64)
-        hid_scales = keep.tile([P, O], U8, name="hid_scales", align_bytes=64)
-        nc.vector.quantize_mx(hid_codes[:].bitcast(FP8X4), hid_scales[:], hid_il[:])
-
-        for b in range(N // P):
-            acc = psum.tile([P, O], F32, name="y%d" % b, tag="bank%d" % b)
-            nc.tensor.matmul_mx(
-                acc[:],
-                lhsT=vs_codes[:, b * P : (b + 1) * P].bitcast(FP8X4),
-                lhsT_scale=vs_planes[:, b * P : (b + 1) * P],
-                rhs=hid_codes[:].bitcast(FP8X4),
-                rhs_scale=hid_scales[:],
-                start=True,
-                stop=True,
-            )
-            res = keep.tile([P, O], F32, name="res%d" % b)
-            if b == 0:
-                nc.vector.tensor_copy(res[:], acc[:])
-                nc.sync.dma_start(out[b * P : (b + 1) * P, :], res[:])
+            if s < PACK - 1:
+                gather(picked[:, s, :], a_win[s], l5[:], sa_t, s)
             else:
-                nc.scalar.copy(res[:], acc[:])
-                nc.scalar.dma_start(out[b * P : (b + 1) * P, :], res[:])
+                for h in range(2):
+                    gather(picked[:, s, h * OH : (h + 1) * OH], a_win[s], l5[:, h * OH // 16 : (h + 1) * OH // 16], sa_t, s)
+
+        res = [keep.tile([P, O], F32, name="res%d" % b) for b in range(N // P)]
+        hid_il = [keep.tile([P, OH * PACK], BF16, name="hid_il%d" % h, align_bytes=64) for h in range(2)]
+        for h in range(2):
+            cols = slice(h * OH, (h + 1) * OH)
+            nc.vector.tensor_tensor(
+                hid_il[h][:].rearrange("p (c i t) -> p c t i", i=2, t=PACK),
+                picked[:, :, cols].rearrange("p t (c i) -> p c t i", i=2),
+                gain[:, :, cols].rearrange("p t (c i) -> p c t i", i=2),
+                MULT,
+            )
+        for h in range(2):
+            cols = slice(h * OH, (h + 1) * OH)
+            hid_codes = keep.tile([P, OH], U32, name="hid_codes%d" % h, align_bytes=64)
+            hid_scales = keep.tile([P, OH], U8, name="hid_scales%d" % h, align_bytes=64)
+            nc.vector.quantize_mx(hid_codes[:].bitcast(FP8X4), hid_scales[:], hid_il[h][:])
+            for b in range(N // P):
+                acc = psum.tile([P, OH], F32, name="y%d%d" % (h, b), tag="bank%d" % (2 * h + b))
+                nc.tensor.matmul_mx(
+                    acc[:],
+                    lhsT=vs_codes[:, b * P : (b + 1) * P].bitcast(FP8X4),
+                    lhsT_scale=vs_planes[:, b * P : (b + 1) * P],
+                    rhs=hid_codes[:].bitcast(FP8X4),
+                    rhs_scale=hid_scales[:],
+                    start=True,
+                    stop=True,
+                )
+                if b == 0:
+                    nc.vector.tensor_copy(res[b][:, cols], acc[:])
+                else:
+                    nc.scalar.copy(res[b][:, cols], acc[:])
+        nc.sync.dma_start(out[0:P, :], res[0][:])
+        nc.scalar.dma_start(out[P : 2 * P, :], res[1][:])

from contextlib import ExitStack

import concourse.mybir as mybir

K, J, R, T, U, F, G, O, D, N, S = 512, 256, 512, 512, 512, 2048, 1024, 128, 512, 256, 1024
FLOPS = 2 * K * R * J + 2 * R * N * O

F32 = mybir.dt.float32
BF16 = mybir.dt.bfloat16
I32 = mybir.dt.int32
U32 = mybir.dt.uint32
U16 = mybir.dt.uint16
U8 = mybir.dt.uint8
FP8X4 = mybir.dt.float8_e4m3fn_x4
COPY = mybir.ActivationFunctionType.Copy
MAX = mybir.AluOpType.max
MULT = mybir.AluOpType.mult

P = 128
PACK = 4
HALF = J // 2
OH = O // 2


def tile_picked_largercode_respelled_one_codedgain_store_plain_kernel(
    tc, ta, tb, ga, gb, ua, ha, hb, tl, sa, sl, vs_words, vs_scales,
    offs, offs2, offs3, offs4, offs5, offs6, offs7, out,
):
    nc = tc.nc
    with ExitStack() as ctx:
        keep = ctx.enter_context(tc.tile_pool(name="keep", bufs=1))
        psum = ctx.enter_context(tc.psum_pool(name="psum", bufs=1))

        def load_list(src, name):
            tile = keep.tile(list(src.shape), U16, name=name)
            nc.sync.dma_start(tile[:], src)
            return tile

        def load_steps(queue, src, name, cols=slice(0, PACK)):
            tile = keep.tile([P, cols.stop - cols.start], F32, name=name)
            queue.dma_start(tile[:], src.rearrange("(p t) o -> p (t o)", t=PACK)[:, cols])
            return tile

        def load_plane(src, t, name):
            tile = keep.tile([P, src.shape[1]], F32, name=name)
            nc.sync.dma_start(tile[:], src.rearrange("(p t) c -> t p c", t=PACK)[t])
            return tile

        def gather(dst, window, offsets, steps, t):
            nc.scalar.activation(dst, window[:].indirect(offsets), COPY, scale=steps[:, t : t + 1])

        scale_win = keep.tile([P, S], U8, name="scale_win")
        nc.vector.memset(scale_win[:].bitcast(I32), 0)

        ta_p = [load_plane(ta, 0, "ta0")]
        l1 = load_list(offs, "l1")
        ga_t = load_steps(nc.scalar, ga, "ga_t")
        ha_t = load_steps(nc.scalar, ha, "ha_t")
        l3 = load_list(offs3, "l3")
        ua_p = [load_plane(ua, t, "ua%d" % t) for t in range(2)]
        l4 = load_list(offs4, "l4")
        hb_t = [load_steps(nc.sync, hb, "hb_lo", cols=slice(0, 2))]
        ua_p.extend(load_plane(ua, t, "ua%d" % t) for t in range(2, PACK))
        l7 = load_list(offs7, "l7")
        scale_rows = keep.tile([4, 4, S // 4], I32, name="scale_rows")
        nc.sync.dma_start(scale_rows[:], vs_scales[0].bitcast(I32).rearrange("(q r) s -> r q s", r=4))
        word_win = keep.tile([P, S], I32, name="word_win")
        nc.sync.dma_start(word_win[:], vs_words[0].rearrange("p s b -> p (s b)").bitcast(I32))
        hb_t.append(load_steps(nc.sync, hb, "hb_hi", cols=slice(2, 4)))
        ta_p.extend(load_plane(ta, t, "ta%d" % t) for t in range(1, PACK))
        gb_t = load_steps(nc.sync, gb, "gb_t")
        tb_p = [load_plane(tb, t, "tb%d" % t) for t in range(PACK)]
        l2 = load_list(offs2, "l2")
        l6 = load_list(offs6, "l6")
        sl_t = load_steps(nc.sync, sl, "sl_t")
        tl_p = [load_plane(tl, t, "tl%d" % t) for t in range(PACK)]
        l5 = load_list(offs5, "l5")
        sa_t = load_steps(nc.sync, sa, "sa_t")

        for q in range(4):
            nc.vector.tensor_copy(scale_win[32 * q : 32 * q + 4, :].bitcast(I32), scale_rows[:, q, :])

        xa = keep.tile([P, PACK, J], F32, name="xa")
        gather(xa[:, 0, :], ta_p[0], l1[:], ga_t, 0)

        vs_codes = keep.tile([P, N], U32, name="vs_codes", align_bytes=64)
        vs_planes = keep.tile([P, N], U8, name="vs_planes", align_bytes=64)
        nc.vector.tensor_copy(vs_codes[:], word_win[:].bitcast(U32).indirect(l7[:]))
        nc.vector.tensor_copy(vs_planes[:], scale_win[:].indirect(l7[:]))

        wc = keep.tile([P, PACK, R], BF16, name="wc")
        wcd = [keep.tile([P, G], F32, name="wcd%d" % t) for t in range(PACK)]
        for pair in range(2):
            for e in range(2):
                gather(wcd[2 * pair + e][:], ua_p[2 * pair + e], l3[:], ha_t, 2 * pair + e)
            for e in range(2):
                gather(wc[:, 2 * pair + e, :], wcd[2 * pair + e], l4[:], hb_t[pair], e)
        wc_il = keep.tile([P, R * PACK], BF16, name="wc_il", align_bytes=64)
        nc.vector.tensor_copy(
            wc_il[:].rearrange("p (s m i t) -> p m s i t", s=PACK, i=2, t=PACK),
            wc[:].rearrange("p t (m i s) -> p m s i t", i=2, s=PACK),
        )
        wc_codes = keep.tile([P, R], U32, name="wc_codes", align_bytes=64)
        wc_scales = keep.tile([P, R], U8, name="wc_scales", align_bytes=64)
        nc.vector.quantize_mx(wc_codes[:].bitcast(FP8X4), wc_scales[:], wc_il[:])

        for t in range(1, PACK):
            gather(xa[:, t, :], ta_p[t], l1[:], ga_t, t)
        xb = keep.tile([P, PACK, J], F32, name="xb")
        a_win = [keep.tile([P, J], F32, name="a%d" % s) for s in range(PACK)]
        a_ps = {}
        for h in range(2):
            cols = slice(h * HALF, (h + 1) * HALF)
            for t in range(PACK):
                gather(xb[:, t, cols], tb_p[t], l2[:, h * HALF // 16 : (h + 1) * HALF // 16], gb_t, t)
            xc_il = keep.tile([P, HALF * PACK], BF16, name="xc_il%d" % h, tag="xc_il", align_bytes=64)
            nc.vector.tensor_tensor(
                xc_il[:].rearrange("p (c i t) -> p c t i", i=2, t=PACK),
                xa[:, :, cols].rearrange("p t (c i) -> p c t i", i=2),
                xb[:, :, cols].rearrange("p t (c i) -> p c t i", i=2),
                MAX,
            )
            xc_codes = keep.tile([P, HALF], U32, name="xc_codes%d" % h, align_bytes=64)
            xc_scales = keep.tile([P, HALF], U8, name="xc_scales%d" % h, align_bytes=64)
            nc.vector.quantize_mx(xc_codes[:].bitcast(FP8X4), xc_scales[:], xc_il[:])
            for s in range(PACK):
                acc = psum.tile([P, HALF], F32, name="acc%d%d" % (h, s), tag="bank%d" % (PACK * h + s))
                nc.tensor.matmul_mx(
                    acc[:],
                    lhsT=wc_codes[:, s * P : (s + 1) * P].bitcast(FP8X4),
                    lhsT_scale=wc_scales[:, s * P : (s + 1) * P],
                    rhs=xc_codes[:].bitcast(FP8X4),
                    rhs_scale=xc_scales[:],
                    start=True,
                    stop=True,
                )
                a_ps[(h, s)] = acc

        gain = keep.tile([P, PACK, O], F32, name="gain")
        for s in range(PACK):
            gather(gain[:, s, :], tl_p[s], l6[:], sl_t, s)

        picked = keep.tile([P, PACK, O], F32, name="picked")
        for s in range(PACK):
            for h in range(2):
                nc.vector.tensor_copy(a_win[s][:, h * HALF : (h + 1) * HALF], a_ps[(h, s)][:])
            if s < PACK - 1:
                gather(picked[:, s, :], a_win[s], l5[:], sa_t, s)
            else:
                for h in range(2):
                    gather(picked[:, s, h * OH : (h + 1) * OH], a_win[s], l5[:, h * OH // 16 : (h + 1) * OH // 16], sa_t, s)

        res = [keep.tile([P, O], F32, name="res%d" % b) for b in range(N // P)]
        hid_il = [keep.tile([P, OH * PACK], BF16, name="hid_il%d" % h, align_bytes=64) for h in range(2)]
        for h in range(2):
            cols = slice(h * OH, (h + 1) * OH)
            nc.vector.tensor_tensor(
                hid_il[h][:].rearrange("p (c i t) -> p c t i", i=2, t=PACK),
                picked[:, :, cols].rearrange("p t (c i) -> p c t i", i=2),
                gain[:, :, cols].rearrange("p t (c i) -> p c t i", i=2),
                MULT,
            )
        for h in range(2):
            cols = slice(h * OH, (h + 1) * OH)
            hid_codes = keep.tile([P, OH], U32, name="hid_codes%d" % h, align_bytes=64)
            hid_scales = keep.tile([P, OH], U8, name="hid_scales%d" % h, align_bytes=64)
            nc.vector.quantize_mx(hid_codes[:].bitcast(FP8X4), hid_scales[:], hid_il[h][:])
            for b in range(N // P):
                acc = psum.tile([P, OH], F32, name="y%d%d" % (h, b), tag="bank%d" % (2 * h + b))
                nc.tensor.matmul_mx(
                    acc[:],
                    lhsT=vs_codes[:, b * P : (b + 1) * P].bitcast(FP8X4),
                    lhsT_scale=vs_planes[:, b * P : (b + 1) * P],
                    rhs=hid_codes[:].bitcast(FP8X4),
                    rhs_scale=hid_scales[:],
                    start=True,
                    stop=True,
                )
                if b == 0:
                    nc.vector.tensor_copy(res[b][:, cols], acc[:])
                else:
                    nc.scalar.copy(res[b][:, cols], acc[:])
        nc.sync.dma_start(out[0:P, :], res[0][:])
        nc.scalar.dma_start(out[P : 2 * P, :], res[1][:])
